import numpy as np
import ml_dtypes


def mxq(x, axis, fmt="e4m3"):
    dtype, down = {"e4m3": (ml_dtypes.float8_e4m3fn, 7), "e5m2": (ml_dtypes.float8_e5m2, 14)}[fmt]
    v = np.moveaxis(np.asarray(x, np.float32).astype(ml_dtypes.bfloat16).astype(np.float64), axis, -1)
    blocks = v.reshape(v.shape[:-1] + (-1, 32))
    amax = np.abs(blocks).max(-1, keepdims=True)
    byte = np.maximum(np.where(amax > 0, np.frexp(amax)[1] - 1 + 127, 0) - down, 1)
    scale = np.exp2(byte - 127.0)
    codes = (blocks / scale).astype(np.float32).astype(dtype).astype(np.float64)
    return np.moveaxis((codes * scale).reshape(v.shape), -1, axis)


WIDE = False


def mx_kscale(k):
    if not WIDE:
        return np.ones(k)
    levels = np.array([10, -10, 5, -5, 0])
    if k % 512:
        return np.exp2(np.random.permutation(np.resize(levels, k // 32))).repeat(32)
    a = np.empty((k // 512, 16))
    for p in range(k // 512):
        a[p, :8] = np.random.permutation(np.resize(levels, 8))
        for g in range(8):
            far = levels[np.abs(levels - a[p, g]) >= 10]
            a[p, g + 8] = far[np.random.randint(len(far))]
    return np.exp2(a.ravel()).repeat(32)


def f64(x):
    return np.asarray(x).astype(np.float64)


def striped(idx):
    return np.tile(idx.reshape(-1, 16).T, (8, 1)).astype(np.uint16)


def unstriped(offs):
    return offs[:16].T.reshape(-1).astype(np.int64)


def gelu(v):
    return 0.5 * v * (1.0 + np.tanh(np.sqrt(2.0 / np.pi) * (v + 0.044715 * v**3)))


K, T, E, C, H, N = 1024, 512, 2, 256, 512, 256


def by_expert(wq, xq):
    return np.concatenate([wq[e].T @ xq[:, e * C:(e + 1) * C] for e in range(E)], axis=1)


def setup_inputs():
    n = np.random.standard_normal
    s = mx_kscale(K)[:, None]
    u = mx_kscale(H)
    return {
        "xT": (n((K, T)) * s).astype(np.float32),
        "w1": (n((E, K, H)) / np.sqrt(K) / s[None] * u[None, None, :]).astype(np.float32),
        "w2": (n((E, H, N)) / np.sqrt(H) / u[None, :, None]).astype(np.float32),
        "gate": np.tile(np.random.uniform(0.2, 1.0, E * C), (N, 1)).astype(np.float32),
        "offs": striped(np.random.permutation(T)[:E * C]),
    }


def reference(xT, w1, w2, gate, offs):
    idx = unstriped(offs)
    xq = mxq(f64(xT)[:, idx], 0, "e4m3")
    h = gelu(by_expert(mxq(f64(w1), 1, "e4m3"), xq))
    y = by_expert(mxq(f64(w2), 1, "e4m3"), mxq(h, 0, "e4m3"))
    out = np.zeros((N, T))
    out[:, idx] = f64(gate) * y
    return out

@@ -1,0 +1,266 @@
+from contextlib import ExitStack
+
+import concourse.mybir as mybir
+
+K, T, E, C, H, N = 1024, 512, 2, 256, 512, 256
+FLOPS = 2 * E * C * (K * H + H * N)
+
+F32 = mybir.dt.float32
+BF16 = mybir.dt.bfloat16
+U32 = mybir.dt.uint32
+U16 = mybir.dt.uint16
+U8 = mybir.dt.uint8
+FP8X4 = mybir.dt.float8_e4m3fn_x4
+MULT = mybir.AluOpType.mult
+ADD = mybir.AluOpType.add
+GELU = mybir.ActivationFunctionType.Gelu_apprx_tanh
+
+P = 128
+PACK = 4
+K_PASS = P * PACK
+PASSES = K // K_PASS
+CHUNK = 128
+CHUNKS = C // CHUNK
+N_TILES = N // P
+
+X_SPLIT = {(0, 0): (("s", 0, 256),), (0, 1): (("s", 0, 256),), (1, 0): (("g", 0, 256),), (1, 1): (("g", 0, 256),)}
+W1_SPLIT = {(e, g): (("s", 0, 64), ("g", 64, 128)) for e in range(E) for g in range(PASSES)}
+W2_SPLIT = {0: (("s", 0, 256),), 1: (("s", 0, 128), ("g", 128, 256))}
+TAGS = {("w1raw", 0, 1): "slotC"}
+JOINT = {1: "slotC"}
+COPY_SCATTER = False
+
+
+def tile_routed_moe_kernel(tc, xT, w1, w2, gate, offs, out):
+    nc = tc.nc
+
+    def spread(split, dst, src):
+        for eng, c0, c1 in split:
+            if eng == "s":
+                nc.scalar.copy(out=dst[:, c0:c1], in_=src[:, c0:c1])
+            elif eng == "v":
+                nc.vector.tensor_copy(out=dst[:, c0:c1], in_=src[:, c0:c1])
+            else:
+                nc.gpsimd.tensor_scalar(out=dst[:, c0:c1], in0=src[:, c0:c1], scalar1=1.0, scalar2=0.0, op0=MULT, op1=ADD)
+
+    def quantize(codes, scales, grouped):
+        nc.vector.quantize_mx(out=codes[:].bitcast(FP8X4), scales=scales[:], in_=grouped)
+
+    with ExitStack() as ctx:
+        lists = ctx.enter_context(tc.tile_pool(name="lists", bufs=1))
+        keep = ctx.enter_context(tc.tile_pool(name="keep", bufs=1))
+        psum = ctx.enter_context(tc.psum_pool(name="psum", bufs=1))
+
+        offsets = lists.tile([P, E * C // 16], U16, name="offsets")
+        nc.sync.dma_start(offsets[:], offs)
+
+        x_view = xT.rearrange("(g p t) n -> g p t n", p=P, t=PACK)
+        gate_view = gate.rearrange("(m p) j -> p m j", p=P)
+        planes = {}
+        w1_raw = {}
+        w2_raw = {}
+        gate_sb = {}
+
+        def load_plane(g, t):
+            planes[g, t] = keep.tile([P, T], F32, name="plane%d%d" % (g, t))
+            nc.sync.dma_start(planes[g, t][:], x_view[g, :, t, :])
+
+        def load_w1(e, g):
+            w1_raw[e, g] = keep.tile([P, PACK, H], F32, name="w1raw%d%d" % (e, g), tag=TAGS.get(("w1raw", e, g), "w1raw%d%d" % (e, g)), align_bytes=64)
+            nc.sync.dma_start(
+                w1_raw[e, g][:],
+                w1[e, g * K_PASS : (g + 1) * K_PASS, :].rearrange("(p j) c -> p j c", j=PACK),
+            )
+
+        def load_w2(e):
+            w2_raw[e] = keep.tile([P, PACK, N], F32, name="w2raw%d" % e)
+            nc.sync.dma_start(w2_raw[e][:], w2[e, :, :].rearrange("(p j) c -> p j c", j=PACK))
+
+        def load_gate(e):
+            gate_sb[e] = keep.tile([P, N_TILES, C], F32, name="gate%d" % e)
+            nc.sync.dma_start(gate_sb[e][:], gate_view[:, :, e * C : (e + 1) * C])
+
+        for g in range(PASSES):
+            for t in range(PACK):
+                load_plane(g, t)
+        for e in range(E):
+            for g in range(PASSES):
+                load_w1(e, g)
+        for e in range(E):
+            load_w2(e)
+        for e in range(E):
+            load_gate(e)
+
+        warm_in = keep.tile([P, 1], F32, name="warm_in")
+        warm_out = keep.tile([P, 1], F32, name="warm_out")
+        nc.gpsimd.memset(warm_in[:], 0.0)
+        nc.scalar.activation(out=warm_out[:], in_=warm_in[:], func=GELU)
+
+        picked = {}
+        joint = {}
+        x_grouped = {}
+        x_codes = {}
+        x_scales = {}
+        w1_grouped = {}
+        w1_codes = {}
+        w1_scales = {}
+        w2_grouped = {}
+        w2_codes = {}
+        w2_scales = {}
+        acc = {}
+        h_grouped = {}
+        h_codes = {}
+        h_scales = {}
+        y_acc = {}
+        y_sb = {}
+        windows = [keep.tile([P, T], F32, name="window%d" % m) for m in range(N_TILES)]
+
+        def alloc_picked(e, g):
+            picked[e, g] = keep.tile([P, PACK, C], F32, name="picked%d%d" % (e, g), tag=TAGS.get(("picked", e, g), "picked%d%d" % (e, g)), align_bytes=64)
+
+        def gather_one(e, g, t):
+            nc.vector.tensor_copy(
+                out=picked[e, g][:, t, :],
+                in_=planes[g, t][:].indirect(offsets[:, e * (C // 16) : (e + 1) * (C // 16)]),
+            )
+
+        def gather(e, g):
+            alloc_picked(e, g)
+            for t in range(PACK):
+                gather_one(e, g, t)
+
+        def il_x(e, g):
+            if g in JOINT:
+                if g not in joint:
+                    joint[g] = keep.tile([P, E, C, PACK], BF16, name="xgj%d" % g, tag=JOINT[g], align_bytes=64)
+                x_grouped[e, g] = joint[g][:, e]
+            else:
+                x_grouped[e, g] = keep.tile([P, C, PACK], BF16, name="xg%d%d" % (e, g), tag=TAGS.get(("xg", e, g), "xg%d%d" % (e, g)), align_bytes=64)
+            spread(X_SPLIT[e, g], x_grouped[e, g][:], picked[e, g][:].rearrange("p t n -> p n t"))
+
+        def q_x(e, g):
+            x_codes[e, g] = keep.tile([P, C], U32, name="xc%d%d" % (e, g), align_bytes=64)
+            x_scales[e, g] = keep.tile([P, C], U8, name="xs%d%d" % (e, g), align_bytes=64)
+            quantize(x_codes[e, g], x_scales[e, g], x_grouped[e, g][:].rearrange("p n t -> p (n t)"))
+
+        def il_w1(e, g):
+            w1_grouped[e, g] = keep.tile([P, H * PACK], BF16, name="w1g%d%d" % (e, g), tag=TAGS.get(("w1g", e, g), "w1g%d%d" % (e, g)), align_bytes=64)
+            spread(
+                W1_SPLIT[e, g],
+                w1_grouped[e, g][:].rearrange("p (t m j) -> p m t j", t=PACK, j=PACK),
+                w1_raw[e, g][:].rearrange("p j (m t) -> p m t j", t=PACK),
+            )
+
+        def q_w1(e, g):
+            w1_codes[e, g] = keep.tile([P, H], U32, name="w1c%d%d" % (e, g), align_bytes=64)
+            w1_scales[e, g] = keep.tile([P, H], U8, name="w1s%d%d" % (e, g), align_bytes=64)
+            quantize(w1_codes[e, g], w1_scales[e, g], w1_grouped[e, g][:])
+
+        def il_w2(e):
+            w2_grouped[e] = keep.tile([P, N, PACK], BF16, name="w2g%d" % e, align_bytes=64)
+            spread(W2_SPLIT[e], w2_grouped[e][:], w2_raw[e][:].rearrange("p j n -> p n j"))
+
+        def q_w2(e):
+            w2_codes[e] = keep.tile([P, N], U32, name="w2c%d" % e, align_bytes=64)
+            w2_scales[e] = keep.tile([P, N], U8, name="w2s%d" % e, align_bytes=64)
+            quantize(w2_codes[e], w2_scales[e], w2_grouped[e][:].rearrange("p n j -> p (n j)"))
+
+        def layer1(e, s):
+            cols = slice(s * CHUNK, (s + 1) * CHUNK)
+            acc[e, s] = psum.tile([P, PACK, CHUNK], F32, name="acc%d%d" % (e, s))
+            for t in range(PACK):
+                feats = slice(t * P, (t + 1) * P)
+                for g in range(PASSES):
+                    nc.tensor.matmul_mx(
+                        out=acc[e, s][:, t, :],
+                        lhsT=w1_codes[e, g][:, feats].bitcast(FP8X4),
+                        lhsT_scale=w1_scales[e, g][:, feats],
+                        rhs=x_codes[e, g][:, cols].bitcast(FP8X4),
+                        rhs_scale=x_scales[e, g][:, cols],
+                        start=(g == 0),
+                        stop=(g == PASSES - 1),
+                    )
+
+        def gelu(e, s):
+            h_grouped[e, s] = keep.tile([P, CHUNK, PACK], BF16, name="hg%d%d" % (e, s), align_bytes=64)
+            nc.scalar.activation(out=h_grouped[e, s][:], in_=acc[e, s][:].rearrange("p t n -> p n t"), func=GELU)
+
+        def q_h(e, s):
+            h_codes[e, s] = keep.tile([P, CHUNK], U32, name="hc%d%d" % (e, s), align_bytes=64)
+            h_scales[e, s] = keep.tile([P, CHUNK], U8, name="hs%d%d" % (e, s), align_bytes=64)
+            quantize(h_codes[e, s], h_scales[e, s], h_grouped[e, s][:].rearrange("p n t -> p (n t)"))
+
+        def layer2(e, s):
+            y_acc[e, s] = psum.tile([P, N_TILES, CHUNK], F32, name="y%d%d" % (e, s))
+            for m in range(N_TILES):
+                feats = slice(m * P, (m + 1) * P)
+                nc.tensor.matmul_mx(
+                    out=y_acc[e, s][:, m, :],
+                    lhsT=w2_codes[e][:, feats].bitcast(FP8X4),
+                    lhsT_scale=w2_scales[e][:, feats],
+                    rhs=h_codes[e, s][:].bitcast(FP8X4),
+                    rhs_scale=h_scales[e, s][:],
+                    start=True,
+                    stop=True,
+                )
+
+        def y_out(e, s):
+            cols = slice(s * CHUNK, (s + 1) * CHUNK)
+            y_sb[e, s] = keep.tile([P, N_TILES, CHUNK], F32, name="ysb%d%d" % (e, s))
+            if COPY_SCATTER:
+                nc.vector.tensor_tensor(out=y_sb[e, s][:], in0=y_acc[e, s][:], in1=gate_sb[e][:, :, cols], op=MULT)
+            else:
+                nc.scalar.copy(out=y_sb[e, s][:], in_=y_acc[e, s][:])
+
+        def scatter(e, s):
+            cols = slice(s * CHUNK, (s + 1) * CHUNK)
+            first = (e * C + s * CHUNK) // 16
+            for m in range(N_TILES):
+                target = windows[m][:].indirect(offsets[:, first : first + CHUNK // 16])
+                if COPY_SCATTER:
+                    nc.vector.tensor_copy(out=target, in_=y_sb[e, s][:, m, :])
+                else:
+                    nc.vector.tensor_tensor(out=target, in0=y_sb[e, s][:, m, :], in1=gate_sb[e][:, m, cols], op=MULT)
+
+        for g in range(PASSES):
+            for e in range(E):
+                alloc_picked(e, g)
+            for t in range(PACK):
+                for e in range(E):
+                    gather_one(e, g, t)
+        for e in range(E):
+            il_x(e, 0)
+        for e in range(E):
+            q_x(e, 0)
+        for g in range(PASSES):
+            il_w1(0, g)
+            q_w1(0, g)
+        for e in range(E):
+            il_x(e, 1)
+        for e in range(E):
+            q_x(e, 1)
+        for s in range(CHUNKS):
+            layer1(0, s)
+            gelu(0, s)
+            q_h(0, s)
+        for g in range(PASSES):
+            il_w1(1, g)
+            q_w1(1, g)
+        for e in range(E):
+            il_w2(e)
+            q_w2(e)
+        for s in range(CHUNKS):
+            layer2(0, s)
+            y_out(0, s)
+        for s in range(CHUNKS):
+            layer1(1, s)
+            gelu(1, s)
+            q_h(1, s)
+            layer2(1, s)
+            y_out(1, s)
+        for e in range(E):
+            for s in range(CHUNKS):
+                scatter(e, s)
+
+        for m in range(N_TILES):
+            nc.sync.dma_start(out[m * P : (m + 1) * P, :], windows[m][:])

@@ -23,11 +23,8 @@ CHUNK = 128
 CHUNKS = C // CHUNK
 N_TILES = N // P
 
-X_SPLIT = {(0, 0): (("s", 0, 256),), (0, 1): (("s", 0, 256),), (1, 0): (("g", 0, 256),), (1, 1): (("g", 0, 256),)}
-W1_SPLIT = {(e, g): (("s", 0, 64), ("g", 64, 128)) for e in range(E) for g in range(PASSES)}
-W2_SPLIT = {0: (("s", 0, 256),), 1: (("s", 0, 128), ("g", 128, 256))}
-TAGS = {("w1raw", 0, 1): "slotC"}
-JOINT = {1: "slotC"}
+W1_SPLIT = {(0, 0): (("s", 0, 128),), (0, 1): (("s", 0, 128),), (1, 0): (("s", 0, 128),), (1, 1): (("s", 0, 64), ("v", 64, 128))}
+W2_SPLIT = {0: (("s", 0, 256),), 1: (("v", 0, 256),)}
 COPY_SCATTER = False
 
 
@@ -44,7 +41,7 @@ def tile_routed_moe_kernel(tc, xT, w1, w2, gate, offs, out):
                 nc.gpsimd.tensor_scalar(out=dst[:, c0:c1], in0=src[:, c0:c1], scalar1=1.0, scalar2=0.0, op0=MULT, op1=ADD)
 
     def quantize(codes, scales, grouped):
-        nc.vector.quantize_mx(out=codes[:].bitcast(FP8X4), scales=scales[:], in_=grouped)
+        nc.vector.quantize_mx(out=codes.bitcast(FP8X4), scales=scales, in_=grouped)
 
     with ExitStack() as ctx:
         lists = ctx.enter_context(tc.tile_pool(name="lists", bufs=1))
@@ -56,17 +53,16 @@ def tile_routed_moe_kernel(tc, xT, w1, w2, gate, offs, out):
 
         x_view = xT.rearrange("(g p t) n -> g p t n", p=P, t=PACK)
         gate_view = gate.rearrange("(m p) j -> p m j", p=P)
-        planes = {}
+        x_raw = [keep.tile([P, PACK, T], F32, name="xraw%d" % g) for g in range(PASSES)]
         w1_raw = {}
         w2_raw = {}
         gate_sb = {}
 
         def load_plane(g, t):
-            planes[g, t] = keep.tile([P, T], F32, name="plane%d%d" % (g, t))
-            nc.sync.dma_start(planes[g, t][:], x_view[g, :, t, :])
+            nc.sync.dma_start(x_raw[g][:, t, :], x_view[g, :, t, :])
 
         def load_w1(e, g):
-            w1_raw[e, g] = keep.tile([P, PACK, H], F32, name="w1raw%d%d" % (e, g), tag=TAGS.get(("w1raw", e, g), "w1raw%d%d" % (e, g)), align_bytes=64)
+            w1_raw[e, g] = keep.tile([P, PACK, H], F32, name="w1raw%d%d" % (e, g))
             nc.sync.dma_start(
                 w1_raw[e, g][:],
                 w1[e, g * K_PASS : (g + 1) * K_PASS, :].rearrange("(p j) c -> p j c", j=PACK),
@@ -96,11 +92,9 @@ def tile_routed_moe_kernel(tc, xT, w1, w2, gate, offs, out):
         nc.gpsimd.memset(warm_in[:], 0.0)
         nc.scalar.activation(out=warm_out[:], in_=warm_in[:], func=GELU)
 
-        picked = {}
-        joint = {}
-        x_grouped = {}
-        x_codes = {}
-        x_scales = {}
+        x_grouped = [keep.tile([P, E, C, PACK], BF16, name="xg%d" % g, align_bytes=64) for g in range(PASSES)]
+        x_codes = [keep.tile([P, E * C], U32, name="xc%d" % g, align_bytes=64) for g in range(PASSES)]
+        x_scales = [keep.tile([P, E * C], U8, name="xs%d" % g, align_bytes=64) for g in range(PASSES)]
         w1_grouped = {}
         w1_codes = {}
         w1_scales = {}
@@ -109,42 +103,23 @@ def tile_routed_moe_kernel(tc, xT, w1, w2, gate, offs, out):
         w2_scales = {}
         acc = {}
         h_grouped = {}
-        h_codes = {}
-        h_scales = {}
+        h_codes = [keep.tile([P, C], U32, name="hc%d" % e, align_bytes=64) for e in range(E)]
+        h_scales = [keep.tile([P, C], U8, name="hs%d" % e, align_bytes=64) for e in range(E)]
         y_acc = {}
         y_sb = {}
         windows = [keep.tile([P, T], F32, name="window%d" % m) for m in range(N_TILES)]
 
-        def alloc_picked(e, g):
-            picked[e, g] = keep.tile([P, PACK, C], F32, name="picked%d%d" % (e, g), tag=TAGS.get(("picked", e, g), "picked%d%d" % (e, g)), align_bytes=64)
-
         def gather_one(e, g, t):
             nc.vector.tensor_copy(
-                out=picked[e, g][:, t, :],
-                in_=planes[g, t][:].indirect(offsets[:, e * (C // 16) : (e + 1) * (C // 16)]),
+                out=x_grouped[g][:, e, :, t],
+                in_=x_raw[g][:, t, :].indirect(offsets[:, e * (C // 16) : (e + 1) * (C // 16)]),
             )
 
-        def gather(e, g):
-            alloc_picked(e, g)
-            for t in range(PACK):
-                gather_one(e, g, t)
-
-        def il_x(e, g):
-            if g in JOINT:
-                if g not in joint:
-                    joint[g] = keep.tile([P, E, C, PACK], BF16, name="xgj%d" % g, tag=JOINT[g], align_bytes=64)
-                x_grouped[e, g] = joint[g][:, e]
-            else:
-                x_grouped[e, g] = keep.tile([P, C, PACK], BF16, name="xg%d%d" % (e, g), tag=TAGS.get(("xg", e, g), "xg%d%d" % (e, g)), align_bytes=64)
-            spread(X_SPLIT[e, g], x_grouped[e, g][:], picked[e, g][:].rearrange("p t n -> p n t"))
-
-        def q_x(e, g):
-            x_codes[e, g] = keep.tile([P, C], U32, name="xc%d%d" % (e, g), align_bytes=64)
-            x_scales[e, g] = keep.tile([P, C], U8, name="xs%d%d" % (e, g), align_bytes=64)
-            quantize(x_codes[e, g], x_scales[e, g], x_grouped[e, g][:].rearrange("p n t -> p (n t)"))
+        def q_x(g):
+            quantize(x_codes[g][:], x_scales[g][:], x_grouped[g][:].rearrange("p e n t -> p (e n t)"))
 
         def il_w1(e, g):
-            w1_grouped[e, g] = keep.tile([P, H * PACK], BF16, name="w1g%d%d" % (e, g), tag=TAGS.get(("w1g", e, g), "w1g%d%d" % (e, g)), align_bytes=64)
+            w1_grouped[e, g] = keep.tile([P, H * PACK], BF16, name="w1g%d%d" % (e, g), align_bytes=64)
             spread(
                 W1_SPLIT[e, g],
                 w1_grouped[e, g][:].rearrange("p (t m j) -> p m t j", t=PACK, j=PACK),
@@ -154,7 +129,7 @@ def tile_routed_moe_kernel(tc, xT, w1, w2, gate, offs, out):
         def q_w1(e, g):
             w1_codes[e, g] = keep.tile([P, H], U32, name="w1c%d%d" % (e, g), align_bytes=64)
             w1_scales[e, g] = keep.tile([P, H], U8, name="w1s%d%d" % (e, g), align_bytes=64)
-            quantize(w1_codes[e, g], w1_scales[e, g], w1_grouped[e, g][:])
+            quantize(w1_codes[e, g][:], w1_scales[e, g][:], w1_grouped[e, g][:])
 
         def il_w2(e):
             w2_grouped[e] = keep.tile([P, N, PACK], BF16, name="w2g%d" % e, align_bytes=64)
@@ -163,10 +138,10 @@ def tile_routed_moe_kernel(tc, xT, w1, w2, gate, offs, out):
         def q_w2(e):
             w2_codes[e] = keep.tile([P, N], U32, name="w2c%d" % e, align_bytes=64)
             w2_scales[e] = keep.tile([P, N], U8, name="w2s%d" % e, align_bytes=64)
-            quantize(w2_codes[e], w2_scales[e], w2_grouped[e][:].rearrange("p n j -> p (n j)"))
+            quantize(w2_codes[e][:], w2_scales[e][:], w2_grouped[e][:].rearrange("p n j -> p (n j)"))
 
         def layer1(e, s):
-            cols = slice(s * CHUNK, (s + 1) * CHUNK)
+            cols = slice(e * C + s * CHUNK, e * C + (s + 1) * CHUNK)
             acc[e, s] = psum.tile([P, PACK, CHUNK], F32, name="acc%d%d" % (e, s))
             for t in range(PACK):
                 feats = slice(t * P, (t + 1) * P)
@@ -175,8 +150,8 @@ def tile_routed_moe_kernel(tc, xT, w1, w2, gate, offs, out):
                         out=acc[e, s][:, t, :],
                         lhsT=w1_codes[e, g][:, feats].bitcast(FP8X4),
                         lhsT_scale=w1_scales[e, g][:, feats],
-                        rhs=x_codes[e, g][:, cols].bitcast(FP8X4),
-                        rhs_scale=x_scales[e, g][:, cols],
+                        rhs=x_codes[g][:, cols].bitcast(FP8X4),
+                        rhs_scale=x_scales[g][:, cols],
                         start=(g == 0),
                         stop=(g == PASSES - 1),
                     )
@@ -186,59 +161,47 @@ def tile_routed_moe_kernel(tc, xT, w1, w2, gate, offs, out):
             nc.scalar.activation(out=h_grouped[e, s][:], in_=acc[e, s][:].rearrange("p t n -> p n t"), func=GELU)
 
         def q_h(e, s):
-            h_codes[e, s] = keep.tile([P, CHUNK], U32, name="hc%d%d" % (e, s), align_bytes=64)
-            h_scales[e, s] = keep.tile([P, CHUNK], U8, name="hs%d%d" % (e, s), align_bytes=64)
-            quantize(h_codes[e, s], h_scales[e, s], h_grouped[e, s][:].rearrange("p n t -> p (n t)"))
+            cols = slice(s * CHUNK, (s + 1) * CHUNK)
+            quantize(h_codes[e][:, cols], h_scales[e][:, cols], h_grouped[e, s][:].rearrange("p n t -> p (n t)"))
 
-        def layer2(e, s):
-            y_acc[e, s] = psum.tile([P, N_TILES, CHUNK], F32, name="y%d%d" % (e, s))
+        def layer2(e, c0, width):
+            y_acc[e, c0] = psum.tile([P, N_TILES, width], F32, name="y%d%d" % (e, c0))
             for m in range(N_TILES):
                 feats = slice(m * P, (m + 1) * P)
                 nc.tensor.matmul_mx(
-                    out=y_acc[e, s][:, m, :],
+                    out=y_acc[e, c0][:, m, :],
                     lhsT=w2_codes[e][:, feats].bitcast(FP8X4),
                     lhsT_scale=w2_scales[e][:, feats],
-                    rhs=h_codes[e, s][:].bitcast(FP8X4),
-                    rhs_scale=h_scales[e, s][:],
+                    rhs=h_codes[e][:, c0 : c0 + width].bitcast(FP8X4),
+                    rhs_scale=h_scales[e][:, c0 : c0 + width],
                     start=True,
                     stop=True,
                 )
 
-        def y_out(e, s):
-            cols = slice(s * CHUNK, (s + 1) * CHUNK)
-            y_sb[e, s] = keep.tile([P, N_TILES, CHUNK], F32, name="ysb%d%d" % (e, s))
+        def y_out(e, c0, width):
+            y_sb[e, c0] = keep.tile([P, N_TILES, width], F32, name="ysb%d%d" % (e, c0))
             if COPY_SCATTER:
-                nc.vector.tensor_tensor(out=y_sb[e, s][:], in0=y_acc[e, s][:], in1=gate_sb[e][:, :, cols], op=MULT)
+                nc.vector.tensor_tensor(out=y_sb[e, c0][:], in0=y_acc[e, c0][:], in1=gate_sb[e][:, :, c0 : c0 + width], op=MULT)
             else:
-                nc.scalar.copy(out=y_sb[e, s][:], in_=y_acc[e, s][:])
+                nc.scalar.copy(out=y_sb[e, c0][:], in_=y_acc[e, c0][:])
 
-        def scatter(e, s):
-            cols = slice(s * CHUNK, (s + 1) * CHUNK)
-            first = (e * C + s * CHUNK) // 16
+        def scatter(e, c0, width):
+            first = (e * C + c0) // 16
             for m in range(N_TILES):
-                target = windows[m][:].indirect(offsets[:, first : first + CHUNK // 16])
+                target = windows[m][:].indirect(offsets[:, first : first + width // 16])
                 if COPY_SCATTER:
-                    nc.vector.tensor_copy(out=target, in_=y_sb[e, s][:, m, :])
+                    nc.vector.tensor_copy(out=target, in_=y_sb[e, c0][:, m, :])
                 else:
-                    nc.vector.tensor_tensor(out=target, in0=y_sb[e, s][:, m, :], in1=gate_sb[e][:, m, cols], op=MULT)
+                    nc.vector.tensor_tensor(out=target, in0=y_sb[e, c0][:, m, :], in1=gate_sb[e][:, m, c0 : c0 + width], op=MULT)
 
         for g in range(PASSES):
-            for e in range(E):
-                alloc_picked(e, g)
             for t in range(PACK):
                 for e in range(E):
                     gather_one(e, g, t)
-        for e in range(E):
-            il_x(e, 0)
-        for e in range(E):
-            q_x(e, 0)
+            q_x(g)
         for g in range(PASSES):
             il_w1(0, g)
             q_w1(0, g)
-        for e in range(E):
-            il_x(e, 1)
-        for e in range(E):
-            q_x(e, 1)
         for s in range(CHUNKS):
             layer1(0, s)
             gelu(0, s)
@@ -249,18 +212,17 @@ def tile_routed_moe_kernel(tc, xT, w1, w2, gate, offs, out):
         for e in range(E):
             il_w2(e)
             q_w2(e)
-        for s in range(CHUNKS):
-            layer2(0, s)
-            y_out(0, s)
+        layer2(0, 0, C)
+        y_out(0, 0, C)
         for s in range(CHUNKS):
             layer1(1, s)
             gelu(1, s)
             q_h(1, s)
-            layer2(1, s)
-            y_out(1, s)
-        for e in range(E):
-            for s in range(CHUNKS):
-                scatter(e, s)
+            layer2(1, s * CHUNK, CHUNK)
+            y_out(1, s * CHUNK, CHUNK)
+        scatter(0, 0, C)
+        for s in range(CHUNKS):
+            scatter(1, s * CHUNK, CHUNK)
 
         for m in range(N_TILES):
             nc.sync.dma_start(out[m * P : (m + 1) * P, :], windows[m][:])

@@ -22,10 +22,13 @@ PASSES = K // K_PASS
 CHUNK = 128
 CHUNKS = C // CHUNK
 N_TILES = N // P
+COPY = mybir.ActivationFunctionType.Copy
+VPASS = 0
+SPASS = 1
 
-W1_SPLIT = {(0, 0): (("s", 0, 128),), (0, 1): (("s", 0, 128),), (1, 0): (("s", 0, 128),), (1, 1): (("s", 0, 64), ("v", 64, 128))}
+W1_SPLIT = {(0, 0): (("s", 0, 64), ("v", 64, 128)), (0, 1): (("s", 0, 48), ("v", 48, 128)), (1, 0): (("s", 0, 80), ("v", 80, 128)), (1, 1): (("s", 0, 48), ("v", 48, 128))}
 W2_SPLIT = {0: (("s", 0, 256),), 1: (("v", 0, 256),)}
-COPY_SCATTER = False
+YTAG = {("hg", 1, 0): "slotY", ("ysb", 0, 0): "slotY", ("w1raw", 1, 1): "slotW", ("hgj", 0): "slotW"}
 
 
 def tile_routed_moe_kernel(tc, xT, w1, w2, gate, offs, out):
@@ -53,16 +56,15 @@ def tile_routed_moe_kernel(tc, xT, w1, w2, gate, offs, out):
 
         x_view = xT.rearrange("(g p t) n -> g p t n", p=P, t=PACK)
         gate_view = gate.rearrange("(m p) j -> p m j", p=P)
-        x_raw = [keep.tile([P, PACK, T], F32, name="xraw%d" % g) for g in range(PASSES)]
+        v_planes = [keep.tile([P, T], F32, name="vplane%d" % t) for t in range(PACK)]
+        s_raw = [keep.tile([P, T], F32, name="sraw%d" % t) for t in range(PACK)]
+        s_planes = keep.tile([P, PACK, T], BF16, name="splanes")
         w1_raw = {}
         w2_raw = {}
         gate_sb = {}
 
-        def load_plane(g, t):
-            nc.sync.dma_start(x_raw[g][:, t, :], x_view[g, :, t, :])
-
         def load_w1(e, g):
-            w1_raw[e, g] = keep.tile([P, PACK, H], F32, name="w1raw%d%d" % (e, g))
+            w1_raw[e, g] = keep.tile([P, PACK, H], F32, name="w1raw%d%d" % (e, g), tag=YTAG.get(("w1raw", e, g), "w1raw%d%d" % (e, g)), align_bytes=64)
             nc.sync.dma_start(
                 w1_raw[e, g][:],
                 w1[e, g * K_PASS : (g + 1) * K_PASS, :].rearrange("(p j) c -> p j c", j=PACK),
@@ -76,9 +78,9 @@ def tile_routed_moe_kernel(tc, xT, w1, w2, gate, offs, out):
             gate_sb[e] = keep.tile([P, N_TILES, C], F32, name="gate%d" % e)
             nc.sync.dma_start(gate_sb[e][:], gate_view[:, :, e * C : (e + 1) * C])
 
-        for g in range(PASSES):
-            for t in range(PACK):
-                load_plane(g, t)
+        for t in range(PACK):
+            nc.sync.dma_start(s_raw[t][:], x_view[SPASS, :, t, :])
+            nc.sync.dma_start(v_planes[t][:], x_view[VPASS, :, t, :])
         for e in range(E):
             for g in range(PASSES):
                 load_w1(e, g)
@@ -92,6 +94,7 @@ def tile_routed_moe_kernel(tc, xT, w1, w2, gate, offs, out):
         nc.gpsimd.memset(warm_in[:], 0.0)
         nc.scalar.activation(out=warm_out[:], in_=warm_in[:], func=GELU)
 
+        picked = [keep.tile([P, PACK, C], F32, name="picked%d" % e) for e in range(E)]
         x_grouped = [keep.tile([P, E, C, PACK], BF16, name="xg%d" % g, align_bytes=64) for g in range(PASSES)]
         x_codes = [keep.tile([P, E * C], U32, name="xc%d" % g, align_bytes=64) for g in range(PASSES)]
         x_scales = [keep.tile([P, E * C], U8, name="xs%d" % g, align_bytes=64) for g in range(PASSES)]
@@ -103,17 +106,27 @@ def tile_routed_moe_kernel(tc, xT, w1, w2, gate, offs, out):
         w2_scales = {}
         acc = {}
         h_grouped = {}
+        h_joint = {}
         h_codes = [keep.tile([P, C], U32, name="hc%d" % e, align_bytes=64) for e in range(E)]
         h_scales = [keep.tile([P, C], U8, name="hs%d" % e, align_bytes=64) for e in range(E)]
         y_acc = {}
         y_sb = {}
         windows = [keep.tile([P, T], F32, name="window%d" % m) for m in range(N_TILES)]
 
-        def gather_one(e, g, t):
-            nc.vector.tensor_copy(
-                out=x_grouped[g][:, e, :, t],
-                in_=x_raw[g][:, t, :].indirect(offsets[:, e * (C // 16) : (e + 1) * (C // 16)]),
-            )
+        def slots_of(e):
+            return offsets[:, e * (C // 16) : (e + 1) * (C // 16)]
+
+        def cast_plane(t):
+            nc.vector.tensor_copy(out=s_planes[:, t, :], in_=s_raw[t][:])
+
+        def s_gather(e, t):
+            nc.scalar.activation(out=x_grouped[SPASS][:, e, :, t], in_=s_planes[:, t, :].indirect(slots_of(e)), func=COPY)
+
+        def v_gather(e, t):
+            nc.vector.tensor_copy(out=picked[e][:, t, :], in_=v_planes[t][:].indirect(slots_of(e)))
+
+        def il_x(e):
+            nc.vector.tensor_copy(out=x_grouped[VPASS][:, e], in_=picked[e][:].rearrange("p t n -> p n t"))
 
         def q_x(g):
             quantize(x_codes[g][:], x_scales[g][:], x_grouped[g][:].rearrange("p e n t -> p (e n t)"))
@@ -157,12 +170,20 @@ def tile_routed_moe_kernel(tc, xT, w1, w2, gate, offs, out):
                     )
 
         def gelu(e, s):
-            h_grouped[e, s] = keep.tile([P, CHUNK, PACK], BF16, name="hg%d%d" % (e, s), align_bytes=64)
+            if ("hgj", e) in YTAG:
+                if e not in h_joint:
+                    h_joint[e] = keep.tile([P, CHUNKS, CHUNK, PACK], BF16, name="hgj%d" % e, tag=YTAG["hgj", e], align_bytes=64)
+                h_grouped[e, s] = h_joint[e][:, s]
+            else:
+                h_grouped[e, s] = keep.tile([P, CHUNK, PACK], BF16, name="hg%d%d" % (e, s), tag=YTAG.get(("hg", e, s), "hg%d%d" % (e, s)), align_bytes=64)
             nc.scalar.activation(out=h_grouped[e, s][:], in_=acc[e, s][:].rearrange("p t n -> p n t"), func=GELU)
 
         def q_h(e, s):
             cols = slice(s * CHUNK, (s + 1) * CHUNK)
             quantize(h_codes[e][:, cols], h_scales[e][:, cols], h_grouped[e, s][:].rearrange("p n t -> p (n t)"))
+
+        def q_h_all(e):
+            quantize(h_codes[e][:], h_scales[e][:], h_joint[e][:].rearrange("p s n t -> p (s n t)"))
 
         def layer2(e, c0, width):
             y_acc[e, c0] = psum.tile([P, N_TILES, width], F32, name="y%d%d" % (e, c0))
@@ -179,47 +200,52 @@ def tile_routed_moe_kernel(tc, xT, w1, w2, gate, offs, out):
                 )
 
         def y_out(e, c0, width):
-            y_sb[e, c0] = keep.tile([P, N_TILES, width], F32, name="ysb%d%d" % (e, c0))
-            if COPY_SCATTER:
-                nc.vector.tensor_tensor(out=y_sb[e, c0][:], in0=y_acc[e, c0][:], in1=gate_sb[e][:, :, c0 : c0 + width], op=MULT)
-            else:
-                nc.scalar.copy(out=y_sb[e, c0][:], in_=y_acc[e, c0][:])
+            y_sb[e, c0] = keep.tile([P, N_TILES, width], F32, name="ysb%d%d" % (e, c0), tag=YTAG.get(("ysb", e, c0), "ysb%d%d" % (e, c0)), align_bytes=64)
+            nc.scalar.copy(out=y_sb[e, c0][:], in_=y_acc[e, c0][:])
 
         def scatter(e, c0, width):
             first = (e * C + c0) // 16
             for m in range(N_TILES):
-                target = windows[m][:].indirect(offsets[:, first : first + width // 16])
-                if COPY_SCATTER:
-                    nc.vector.tensor_copy(out=target, in_=y_sb[e, c0][:, m, :])
-                else:
-                    nc.vector.tensor_tensor(out=target, in0=y_sb[e, c0][:, m, :], in1=gate_sb[e][:, m, c0 : c0 + width], op=MULT)
+                nc.vector.tensor_tensor(
+                    out=windows[m][:].indirect(offsets[:, first : first + width // 16]),
+                    in0=y_sb[e, c0][:, m, :],
+                    in1=gate_sb[e][:, m, c0 : c0 + width],
+                    op=MULT,
+                )
 
-        for g in range(PASSES):
-            for t in range(PACK):
-                for e in range(E):
-                    gather_one(e, g, t)
-            q_x(g)
-        for g in range(PASSES):
-            il_w1(0, g)
-            q_w1(0, g)
+        for t in range(PACK):
+            cast_plane(t)
+            for e in range(E):
+                s_gather(e, t)
+            for e in range(E):
+                v_gather(e, t)
+        for e in range(E):
+            il_x(e)
+        q_x(VPASS)
+        q_x(SPASS)
+        for e in range(E):
+            for g in range(PASSES):
+                il_w1(e, g)
+                q_w1(e, g)
         for s in range(CHUNKS):
             layer1(0, s)
             gelu(0, s)
-            q_h(0, s)
-        for g in range(PASSES):
-            il_w1(1, g)
-            q_w1(1, g)
+        q_h_all(0)
         for e in range(E):
             il_w2(e)
             q_w2(e)
         layer2(0, 0, C)
+        layer1(1, 0)
+        gelu(1, 0)
+        q_h(1, 0)
         y_out(0, 0, C)
-        for s in range(CHUNKS):
-            layer1(1, s)
-            gelu(1, s)
-            q_h(1, s)
-            layer2(1, s * CHUNK, CHUNK)
-            y_out(1, s * CHUNK, CHUNK)
+        layer2(1, 0, CHUNK)
+        y_out(1, 0, CHUNK)
+        layer1(1, 1)
+        gelu(1, 1)
+        q_h(1, 1)
+        layer2(1, CHUNK, CHUNK)
+        y_out(1, CHUNK, CHUNK)
         scatter(0, 0, C)
         for s in range(CHUNKS):
             scatter(1, s * CHUNK, CHUNK)

@@ -26,7 +26,7 @@ COPY = mybir.ActivationFunctionType.Copy
 VPASS = 0
 SPASS = 1
 
-W1_SPLIT = {(0, 0): (("s", 0, 64), ("v", 64, 128)), (0, 1): (("s", 0, 48), ("v", 48, 128)), (1, 0): (("s", 0, 80), ("v", 80, 128)), (1, 1): (("s", 0, 48), ("v", 48, 128))}
+W1_SPLIT = {(0, 0): (("v", 0, 128),), (0, 1): (("s", 0, 88), ("v", 88, 128)), (1, 0): (("s", 0, 96), ("v", 96, 128)), (1, 1): (("s", 0, 56), ("v", 56, 128))}
 W2_SPLIT = {0: (("s", 0, 256),), 1: (("v", 0, 256),)}
 YTAG = {("hg", 1, 0): "slotY", ("ysb", 0, 0): "slotY", ("w1raw", 1, 1): "slotW", ("hgj", 0): "slotW"}
 
@@ -79,8 +79,8 @@ def tile_routed_moe_kernel(tc, xT, w1, w2, gate, offs, out):
             nc.sync.dma_start(gate_sb[e][:], gate_view[:, :, e * C : (e + 1) * C])
 
         for t in range(PACK):
-            nc.sync.dma_start(s_raw[t][:], x_view[SPASS, :, t, :])
             nc.sync.dma_start(v_planes[t][:], x_view[VPASS, :, t, :])
+            nc.sync.dma_start(s_raw[t][:], x_view[SPASS, :, t, :])
         for e in range(E):
             for g in range(PASSES):
                 load_w1(e, g)
@@ -94,7 +94,7 @@ def tile_routed_moe_kernel(tc, xT, w1, w2, gate, offs, out):
         nc.gpsimd.memset(warm_in[:], 0.0)
         nc.scalar.activation(out=warm_out[:], in_=warm_in[:], func=GELU)
 
-        picked = [keep.tile([P, PACK, C], F32, name="picked%d" % e) for e in range(E)]
+        picked = keep.tile([P, E, PACK, C], F32, name="picked")
         x_grouped = [keep.tile([P, E, C, PACK], BF16, name="xg%d" % g, align_bytes=64) for g in range(PASSES)]
         x_codes = [keep.tile([P, E * C], U32, name="xc%d" % g, align_bytes=64) for g in range(PASSES)]
         x_scales = [keep.tile([P, E * C], U8, name="xs%d" % g, align_bytes=64) for g in range(PASSES)]
@@ -117,16 +117,16 @@ def tile_routed_moe_kernel(tc, xT, w1, w2, gate, offs, out):
             return offsets[:, e * (C // 16) : (e + 1) * (C // 16)]
 
         def cast_plane(t):
-            nc.vector.tensor_copy(out=s_planes[:, t, :], in_=s_raw[t][:])
+            nc.gpsimd.tensor_scalar(out=s_planes[:, t, :], in0=s_raw[t][:], scalar1=1.0, scalar2=0.0, op0=MULT, op1=ADD)
 
         def s_gather(e, t):
             nc.scalar.activation(out=x_grouped[SPASS][:, e, :, t], in_=s_planes[:, t, :].indirect(slots_of(e)), func=COPY)
 
         def v_gather(e, t):
-            nc.vector.tensor_copy(out=picked[e][:, t, :], in_=v_planes[t][:].indirect(slots_of(e)))
+            nc.vector.tensor_copy(out=picked[:, e, t, :], in_=v_planes[t][:].indirect(slots_of(e)))
 
-        def il_x(e):
-            nc.vector.tensor_copy(out=x_grouped[VPASS][:, e], in_=picked[e][:].rearrange("p t n -> p n t"))
+        def il_x_all():
+            nc.vector.tensor_copy(out=x_grouped[VPASS][:], in_=picked[:].rearrange("p e t n -> p e n t"))
 
         def q_x(g):
             quantize(x_codes[g][:], x_scales[g][:], x_grouped[g][:].rearrange("p e n t -> p (e n t)"))
@@ -214,13 +214,12 @@ def tile_routed_moe_kernel(tc, xT, w1, w2, gate, offs, out):
                 )
 
         for t in range(PACK):
+            for e in range(E):
+                v_gather(e, t)
             cast_plane(t)
             for e in range(E):
                 s_gather(e, t)
-            for e in range(E):
-                v_gather(e, t)
-        for e in range(E):
-            il_x(e)
+        il_x_all()
         q_x(VPASS)
         q_x(SPASS)
         for e in range(E):

@@ -26,8 +26,8 @@ COPY = mybir.ActivationFunctionType.Copy
 VPASS = 0
 SPASS = 1
 
-W1_SPLIT = {(0, 0): (("v", 0, 128),), (0, 1): (("s", 0, 88), ("v", 88, 128)), (1, 0): (("s", 0, 96), ("v", 96, 128)), (1, 1): (("s", 0, 56), ("v", 56, 128))}
-W2_SPLIT = {0: (("s", 0, 256),), 1: (("v", 0, 256),)}
+W1_SPLIT = {(0, 0): (("v", 0, 128),), (0, 1): (("s", 0, 80), ("v", 80, 128)), (1, 0): (("s", 0, 64), ("v", 64, 128)), (1, 1): (("s", 0, 40), ("v", 40, 128))}
+W2_SPLIT = {0: (("v", 0, 256),), 1: (("v", 0, 256),)}
 YTAG = {("hg", 1, 0): "slotY", ("ysb", 0, 0): "slotY", ("w1raw", 1, 1): "slotW", ("hgj", 0): "slotW"}
 
 

@@ -56,12 +56,15 @@ def tile_routed_moe_kernel(tc, xT, w1, w2, gate, offs, out):
 
         x_view = xT.rearrange("(g p t) n -> g p t n", p=P, t=PACK)
         gate_view = gate.rearrange("(m p) j -> p m j", p=P)
-        v_planes = [keep.tile([P, T], F32, name="vplane%d" % t) for t in range(PACK)]
+        v_raw = keep.tile([P, PACK * T], F32, name="vraw")
         s_raw = [keep.tile([P, T], F32, name="sraw%d" % t) for t in range(PACK)]
         s_planes = keep.tile([P, PACK, T], BF16, name="splanes")
         w1_raw = {}
         w2_raw = {}
         gate_sb = {}
+
+        def v_slot(t):
+            return PACK - 1 - t
 
         def load_w1(e, g):
             w1_raw[e, g] = keep.tile([P, PACK, H], F32, name="w1raw%d%d" % (e, g), tag=YTAG.get(("w1raw", e, g), "w1raw%d%d" % (e, g)), align_bytes=64)
@@ -79,7 +82,7 @@ def tile_routed_moe_kernel(tc, xT, w1, w2, gate, offs, out):
             nc.sync.dma_start(gate_sb[e][:], gate_view[:, :, e * C : (e + 1) * C])
 
         for t in range(PACK):
-            nc.sync.dma_start(v_planes[t][:], x_view[VPASS, :, t, :])
+            nc.sync.dma_start(v_raw[:, v_slot(t) * T : (v_slot(t) + 1) * T], x_view[VPASS, :, t, :])
             nc.sync.dma_start(s_raw[t][:], x_view[SPASS, :, t, :])
         for e in range(E):
             for g in range(PASSES):
@@ -94,7 +97,7 @@ def tile_routed_moe_kernel(tc, xT, w1, w2, gate, offs, out):
         nc.gpsimd.memset(warm_in[:], 0.0)
         nc.scalar.activation(out=warm_out[:], in_=warm_in[:], func=GELU)
 
-        picked = keep.tile([P, E, PACK, C], F32, name="picked")
+        picked = keep.tile([P, PACK, E * C], F32, name="picked")
         x_grouped = [keep.tile([P, E, C, PACK], BF16, name="xg%d" % g, align_bytes=64) for g in range(PASSES)]
         x_codes = [keep.tile([P, E * C], U32, name="xc%d" % g, align_bytes=64) for g in range(PASSES)]
         x_scales = [keep.tile([P, E * C], U8, name="xs%d" % g, align_bytes=64) for g in range(PASSES)]
@@ -122,11 +125,16 @@ def tile_routed_moe_kernel(tc, xT, w1, w2, gate, offs, out):
         def s_gather(e, t):
             nc.scalar.activation(out=x_grouped[SPASS][:, e, :, t], in_=s_planes[:, t, :].indirect(slots_of(e)), func=COPY)
 
-        def v_gather(e, t):
-            nc.vector.tensor_copy(out=picked[:, e, t, :], in_=v_planes[t][:].indirect(slots_of(e)))
+        def v_gather(t):
+            first = v_slot(t) * T
+            if t == 0:
+                for e in range(E):
+                    nc.vector.tensor_copy(out=picked[:, t, e * C : (e + 1) * C], in_=v_raw[:, first : first + T].indirect(slots_of(e)))
+            else:
+                nc.vector.tensor_copy(out=picked[:, t, :], in_=v_raw[:, first : first + 2 * T].indirect(offsets[:]))
 
         def il_x_all():
-            nc.vector.tensor_copy(out=x_grouped[VPASS][:], in_=picked[:].rearrange("p e t n -> p e n t"))
+            nc.vector.tensor_copy(out=x_grouped[VPASS][:].rearrange("p e n t -> p (e n) t"), in_=picked[:].rearrange("p t n -> p n t"))
 
         def q_x(g):
             quantize(x_codes[g][:], x_scales[g][:], x_grouped[g][:].rearrange("p e n t -> p (e n t)"))
@@ -214,8 +222,7 @@ def tile_routed_moe_kernel(tc, xT, w1, w2, gate, offs, out):
                 )
 
         for t in range(PACK):
-            for e in range(E):
-                v_gather(e, t)
+            v_gather(t)
             cast_plane(t)
             for e in range(E):
                 s_gather(e, t)

@@ -27,7 +27,7 @@ VPASS = 0
 SPASS = 1
 
 W1_SPLIT = {(0, 0): (("v", 0, 128),), (0, 1): (("s", 0, 80), ("v", 80, 128)), (1, 0): (("s", 0, 64), ("v", 64, 128)), (1, 1): (("s", 0, 40), ("v", 40, 128))}
-W2_SPLIT = {0: (("v", 0, 256),), 1: (("v", 0, 256),)}
+W2_SPLIT = {0: (("v", 0, 64),), 1: (("v", 0, 64),)}
 YTAG = {("hg", 1, 0): "slotY", ("ysb", 0, 0): "slotY", ("w1raw", 1, 1): "slotW", ("hgj", 0): "slotW"}
 
 
@@ -134,7 +134,10 @@ def tile_routed_moe_kernel(tc, xT, w1, w2, gate, offs, out):
                 nc.vector.tensor_copy(out=picked[:, t, :], in_=v_raw[:, first : first + 2 * T].indirect(offsets[:]))
 
         def il_x_all():
-            nc.vector.tensor_copy(out=x_grouped[VPASS][:].rearrange("p e n t -> p (e n) t"), in_=picked[:].rearrange("p t n -> p n t"))
+            nc.vector.tensor_copy(
+                out=x_grouped[VPASS][:].rearrange("p e n t -> p (e n) t").rearrange("p (c i) t -> p c t i", i=PACK),
+                in_=picked[:].rearrange("p t (c i) -> p c t i", i=PACK),
+            )
 
         def q_x(g):
             quantize(x_codes[g][:], x_scales[g][:], x_grouped[g][:].rearrange("p e n t -> p (e n t)"))
@@ -143,8 +146,8 @@ def tile_routed_moe_kernel(tc, xT, w1, w2, gate, offs, out):
             w1_grouped[e, g] = keep.tile([P, H * PACK], BF16, name="w1g%d%d" % (e, g), align_bytes=64)
             spread(
                 W1_SPLIT[e, g],
-                w1_grouped[e, g][:].rearrange("p (t m j) -> p m t j", t=PACK, j=PACK),
-                w1_raw[e, g][:].rearrange("p j (m t) -> p m t j", t=PACK),
+                w1_grouped[e, g][:].rearrange("p (t m j) -> p m j t", t=PACK, j=PACK),
+                w1_raw[e, g][:].rearrange("p j (m t) -> p m j t", t=PACK),
             )
 
         def q_w1(e, g):
@@ -154,7 +157,11 @@ def tile_routed_moe_kernel(tc, xT, w1, w2, gate, offs, out):
 
         def il_w2(e):
             w2_grouped[e] = keep.tile([P, N, PACK], BF16, name="w2g%d" % e, align_bytes=64)
-            spread(W2_SPLIT[e], w2_grouped[e][:], w2_raw[e][:].rearrange("p j n -> p n j"))
+            spread(
+                W2_SPLIT[e],
+                w2_grouped[e][:].rearrange("p (c i) j -> p c j i", i=PACK),
+                w2_raw[e][:].rearrange("p j (c i) -> p c j i", i=PACK),
+            )
 
         def q_w2(e):
             w2_codes[e] = keep.tile([P, N], U32, name="w2c%d" % e, align_bytes=64)

@@ -28,7 +28,7 @@ SPASS = 1
 
 W1_SPLIT = {(0, 0): (("v", 0, 128),), (0, 1): (("s", 0, 80), ("v", 80, 128)), (1, 0): (("s", 0, 64), ("v", 64, 128)), (1, 1): (("s", 0, 40), ("v", 40, 128))}
 W2_SPLIT = {0: (("v", 0, 64),), 1: (("v", 0, 64),)}
-YTAG = {("hg", 1, 0): "slotY", ("ysb", 0, 0): "slotY", ("w1raw", 1, 1): "slotW", ("hgj", 0): "slotW"}
+YTAG = {("hgj", 1): "hgj1", ("w1raw", 1, 1): "slotW", ("hgj", 0): "slotW"}
 
 
 def tile_routed_moe_kernel(tc, xT, w1, w2, gate, offs, out):
@@ -218,6 +218,31 @@ def tile_routed_moe_kernel(tc, xT, w1, w2, gate, offs, out):
             y_sb[e, c0] = keep.tile([P, N_TILES, width], F32, name="ysb%d%d" % (e, c0), tag=YTAG.get(("ysb", e, c0), "ysb%d%d" % (e, c0)), align_bytes=64)
             nc.scalar.copy(out=y_sb[e, c0][:], in_=y_acc[e, c0][:])
 
+        def layer2_half(e, m, tag):
+            feats = slice(m * P, (m + 1) * P)
+            y_acc[e, m] = psum.tile([P, C], F32, name="yh%d%d" % (e, m), tag=tag)
+            nc.tensor.matmul_mx(
+                out=y_acc[e, m][:],
+                lhsT=w2_codes[e][:, feats].bitcast(FP8X4),
+                lhsT_scale=w2_scales[e][:, feats],
+                rhs=h_codes[e][:].bitcast(FP8X4),
+                rhs_scale=h_scales[e][:],
+                start=True,
+                stop=True,
+            )
+
+        def y_out_half(e, m, tag):
+            y_sb[e, m] = keep.tile([P, C], F32, name="ysbh%d%d" % (e, m), tag=tag)
+            nc.scalar.copy(out=y_sb[e, m][:], in_=y_acc[e, m][:])
+
+        def scatter_half(e, m):
+            nc.vector.tensor_tensor(
+                out=windows[m][:].indirect(slots_of(e)),
+                in0=y_sb[e, m][:],
+                in1=gate_sb[e][:, m, :],
+                op=MULT,
+            )
+
         def scatter(e, c0, width):
             first = (e * C + c0) // 16
             for m in range(N_TILES):
@@ -247,21 +272,19 @@ def tile_routed_moe_kernel(tc, xT, w1, w2, gate, offs, out):
         for e in range(E):
             il_w2(e)
             q_w2(e)
-        layer2(0, 0, C)
-        layer1(1, 0)
-        gelu(1, 0)
-        q_h(1, 0)
-        y_out(0, 0, C)
-        layer2(1, 0, CHUNK)
-        y_out(1, 0, CHUNK)
-        layer1(1, 1)
-        gelu(1, 1)
-        q_h(1, 1)
-        layer2(1, CHUNK, CHUNK)
-        y_out(1, CHUNK, CHUNK)
-        scatter(0, 0, C)
+        layer2_half(0, 0, "yh00")
+        y_out_half(0, 0, "w2raw1")
         for s in range(CHUNKS):
-            scatter(1, s * CHUNK, CHUNK)
+            layer1(1, s)
+            gelu(1, s)
+        q_h_all(1)
+        layer2_half(0, 1, "acc11")
+        y_out_half(0, 1, "ysbh01")
+        layer2(1, 0, C)
+        y_out(1, 0, C)
+        scatter_half(0, 0)
+        scatter_half(0, 1)
+        scatter(1, 0, C)
 
         for m in range(N_TILES):
             nc.sync.dma_start(out[m * P : (m + 1) * P, :], windows[m][:])

@@ -56,7 +56,8 @@ def tile_routed_moe_kernel(tc, xT, w1, w2, gate, offs, out):
 
         x_view = xT.rearrange("(g p t) n -> g p t n", p=P, t=PACK)
         gate_view = gate.rearrange("(m p) j -> p m j", p=P)
-        v_raw = keep.tile([P, PACK * T], F32, name="vraw")
+        v_raw = keep.tile([P, (PACK + 1) * T], F32, name="vraw")
+        nc.gpsimd.memset(v_raw[:, PACK * T :], 0.0)
         s_raw = [keep.tile([P, T], F32, name="sraw%d" % t) for t in range(PACK)]
         s_planes = keep.tile([P, PACK, T], BF16, name="splanes")
         w1_raw = {}
@@ -127,11 +128,7 @@ def tile_routed_moe_kernel(tc, xT, w1, w2, gate, offs, out):
 
         def v_gather(t):
             first = v_slot(t) * T
-            if t == 0:
-                for e in range(E):
-                    nc.vector.tensor_copy(out=picked[:, t, e * C : (e + 1) * C], in_=v_raw[:, first : first + T].indirect(slots_of(e)))
-            else:
-                nc.vector.tensor_copy(out=picked[:, t, :], in_=v_raw[:, first : first + 2 * T].indirect(offsets[:]))
+            nc.vector.tensor_copy(out=picked[:, t, :], in_=v_raw[:, first : first + 2 * T].indirect(offsets[:]))
 
         def il_x_all():
             nc.vector.tensor_copy(

@@ -26,8 +26,9 @@ COPY = mybir.ActivationFunctionType.Copy
 VPASS = 0
 SPASS = 1
 
-W1_SPLIT = {(0, 0): (("v", 0, 128),), (0, 1): (("s", 0, 80), ("v", 80, 128)), (1, 0): (("s", 0, 64), ("v", 64, 128)), (1, 1): (("s", 0, 40), ("v", 40, 128))}
-W2_SPLIT = {0: (("v", 0, 64),), 1: (("v", 0, 64),)}
+W1_SPLIT = {(0, 0): (("v", 0, 64),), (0, 1): (("s", 0, 40), ("v", 40, 64)), (1, 0): (("s", 0, 32), ("v", 32, 64)), (1, 1): (("s", 0, 20), ("v", 20, 64))}
+W2_SPLIT = {0: (("v", 0, 32),), 1: (("v", 0, 32),)}
+RUN = 8
 YTAG = {("hgj", 1): "hgj1", ("w1raw", 1, 1): "slotW", ("hgj", 0): "slotW"}
 
 
@@ -132,8 +133,8 @@ def tile_routed_moe_kernel(tc, xT, w1, w2, gate, offs, out):
 
         def il_x_all():
             nc.vector.tensor_copy(
-                out=x_grouped[VPASS][:].rearrange("p e n t -> p (e n) t").rearrange("p (c i) t -> p c t i", i=PACK),
-                in_=picked[:].rearrange("p t (c i) -> p c t i", i=PACK),
+                out=x_grouped[VPASS][:].rearrange("p e n t -> p (e n) t").rearrange("p (c i) t -> p c t i", i=RUN),
+                in_=picked[:].rearrange("p t (c i) -> p c t i", i=RUN),
             )
 
         def q_x(g):
@@ -143,8 +144,8 @@ def tile_routed_moe_kernel(tc, xT, w1, w2, gate, offs, out):
             w1_grouped[e, g] = keep.tile([P, H * PACK], BF16, name="w1g%d%d" % (e, g), align_bytes=64)
             spread(
                 W1_SPLIT[e, g],
-                w1_grouped[e, g][:].rearrange("p (t m j) -> p m j t", t=PACK, j=PACK),
-                w1_raw[e, g][:].rearrange("p j (m t) -> p m j t", t=PACK),
+                w1_grouped[e, g][:].rearrange("p (t m u j) -> p m j u t", t=PACK, u=2, j=PACK),
+                w1_raw[e, g][:].rearrange("p j (m u t) -> p m j u t", u=2, t=PACK),
             )
 
         def q_w1(e, g):
@@ -156,8 +157,8 @@ def tile_routed_moe_kernel(tc, xT, w1, w2, gate, offs, out):
             w2_grouped[e] = keep.tile([P, N, PACK], BF16, name="w2g%d" % e, align_bytes=64)
             spread(
                 W2_SPLIT[e],
-                w2_grouped[e][:].rearrange("p (c i) j -> p c j i", i=PACK),
-                w2_raw[e][:].rearrange("p j (c i) -> p c j i", i=PACK),
+                w2_grouped[e][:].rearrange("p (c i) j -> p c j i", i=RUN),
+                w2_raw[e][:].rearrange("p j (c i) -> p c j i", i=RUN),
             )
 
         def q_w2(e):

from contextlib import ExitStack

import concourse.mybir as mybir

K, T, E, C, H, N = 1024, 512, 2, 256, 512, 256
FLOPS = 2 * E * C * (K * H + H * N)

F32 = mybir.dt.float32
BF16 = mybir.dt.bfloat16
U32 = mybir.dt.uint32
U16 = mybir.dt.uint16
U8 = mybir.dt.uint8
FP8X4 = mybir.dt.float8_e4m3fn_x4
MULT = mybir.AluOpType.mult
ADD = mybir.AluOpType.add
GELU = mybir.ActivationFunctionType.Gelu_apprx_tanh

P = 128
PACK = 4
K_PASS = P * PACK
PASSES = K // K_PASS
CHUNK = 128
CHUNKS = C // CHUNK
N_TILES = N // P
COPY = mybir.ActivationFunctionType.Copy
VPASS = 0
SPASS = 1

W1_SPLIT = {(0, 0): (("v", 0, 64),), (0, 1): (("s", 0, 40), ("v", 40, 64)), (1, 0): (("s", 0, 32), ("v", 32, 64)), (1, 1): (("s", 0, 20), ("v", 20, 64))}
W2_SPLIT = {0: (("v", 0, 32),), 1: (("v", 0, 32),)}
RUN = 8
YTAG = {("hgj", 1): "hgj1", ("w1raw", 1, 1): "slotW", ("hgj", 0): "slotW"}


def tile_routed_moe_kernel(tc, xT, w1, w2, gate, offs, out):
    nc = tc.nc

    def spread(split, dst, src):
        for eng, c0, c1 in split:
            if eng == "s":
                nc.scalar.copy(out=dst[:, c0:c1], in_=src[:, c0:c1])
            elif eng == "v":
                nc.vector.tensor_copy(out=dst[:, c0:c1], in_=src[:, c0:c1])
            else:
                nc.gpsimd.tensor_scalar(out=dst[:, c0:c1], in0=src[:, c0:c1], scalar1=1.0, scalar2=0.0, op0=MULT, op1=ADD)

    def quantize(codes, scales, grouped):
        nc.vector.quantize_mx(out=codes.bitcast(FP8X4), scales=scales, in_=grouped)

    with ExitStack() as ctx:
        lists = ctx.enter_context(tc.tile_pool(name="lists", bufs=1))
        keep = ctx.enter_context(tc.tile_pool(name="keep", bufs=1))
        psum = ctx.enter_context(tc.psum_pool(name="psum", bufs=1))

        offsets = lists.tile([P, E * C // 16], U16, name="offsets")
        nc.sync.dma_start(offsets[:], offs)

        x_view = xT.rearrange("(g p t) n -> g p t n", p=P, t=PACK)
        gate_view = gate.rearrange("(m p) j -> p m j", p=P)
        v_raw = keep.tile([P, (PACK + 1) * T], F32, name="vraw")
        nc.gpsimd.memset(v_raw[:, PACK * T :], 0.0)
        s_raw = [keep.tile([P, T], F32, name="sraw%d" % t) for t in range(PACK)]
        s_planes = keep.tile([P, PACK, T], BF16, name="splanes")
        w1_raw = {}
        w2_raw = {}
        gate_sb = {}

        def v_slot(t):
            return PACK - 1 - t

        def load_w1(e, g):
            w1_raw[e, g] = keep.tile([P, PACK, H], F32, name="w1raw%d%d" % (e, g), tag=YTAG.get(("w1raw", e, g), "w1raw%d%d" % (e, g)), align_bytes=64)
            nc.sync.dma_start(
                w1_raw[e, g][:],
                w1[e, g * K_PASS : (g + 1) * K_PASS, :].rearrange("(p j) c -> p j c", j=PACK),
            )

        def load_w2(e):
            w2_raw[e] = keep.tile([P, PACK, N], F32, name="w2raw%d" % e)
            nc.sync.dma_start(w2_raw[e][:], w2[e, :, :].rearrange("(p j) c -> p j c", j=PACK))

        def load_gate(e):
            gate_sb[e] = keep.tile([P, N_TILES, C], F32, name="gate%d" % e)
            nc.sync.dma_start(gate_sb[e][:], gate_view[:, :, e * C : (e + 1) * C])

        for t in range(PACK):
            nc.sync.dma_start(v_raw[:, v_slot(t) * T : (v_slot(t) + 1) * T], x_view[VPASS, :, t, :])
            nc.sync.dma_start(s_raw[t][:], x_view[SPASS, :, t, :])
        for e in range(E):
            for g in range(PASSES):
                load_w1(e, g)
        for e in range(E):
            load_w2(e)
        for e in range(E):
            load_gate(e)

        warm_in = keep.tile([P, 1], F32, name="warm_in")
        warm_out = keep.tile([P, 1], F32, name="warm_out")
        nc.gpsimd.memset(warm_in[:], 0.0)
        nc.scalar.activation(out=warm_out[:], in_=warm_in[:], func=GELU)

        picked = keep.tile([P, PACK, E * C], F32, name="picked")
        x_grouped = [keep.tile([P, E, C, PACK], BF16, name="xg%d" % g, align_bytes=64) for g in range(PASSES)]
        x_codes = [keep.tile([P, E * C], U32, name="xc%d" % g, align_bytes=64) for g in range(PASSES)]
        x_scales = [keep.tile([P, E * C], U8, name="xs%d" % g, align_bytes=64) for g in range(PASSES)]
        w1_grouped = {}
        w1_codes = {}
        w1_scales = {}
        w2_grouped = {}
        w2_codes = {}
        w2_scales = {}
        acc = {}
        h_grouped = {}
        h_joint = {}
        h_codes = [keep.tile([P, C], U32, name="hc%d" % e, align_bytes=64) for e in range(E)]
        h_scales = [keep.tile([P, C], U8, name="hs%d" % e, align_bytes=64) for e in range(E)]
        y_acc = {}
        y_sb = {}
        windows = [keep.tile([P, T], F32, name="window%d" % m) for m in range(N_TILES)]

        def slots_of(e):
            return offsets[:, e * (C // 16) : (e + 1) * (C // 16)]

        def cast_plane(t):
            nc.gpsimd.tensor_scalar(out=s_planes[:, t, :], in0=s_raw[t][:], scalar1=1.0, scalar2=0.0, op0=MULT, op1=ADD)

        def s_gather(e, t):
            nc.scalar.activation(out=x_grouped[SPASS][:, e, :, t], in_=s_planes[:, t, :].indirect(slots_of(e)), func=COPY)

        def v_gather(t):
            first = v_slot(t) * T
            nc.vector.tensor_copy(out=picked[:, t, :], in_=v_raw[:, first : first + 2 * T].indirect(offsets[:]))

        def il_x_all():
            nc.vector.tensor_copy(
                out=x_grouped[VPASS][:].rearrange("p e n t -> p (e n) t").rearrange("p (c i) t -> p c t i", i=RUN),
                in_=picked[:].rearrange("p t (c i) -> p c t i", i=RUN),
            )

        def q_x(g):
            quantize(x_codes[g][:], x_scales[g][:], x_grouped[g][:].rearrange("p e n t -> p (e n t)"))

        def il_w1(e, g):
            w1_grouped[e, g] = keep.tile([P, H * PACK], BF16, name="w1g%d%d" % (e, g), align_bytes=64)
            spread(
                W1_SPLIT[e, g],
                w1_grouped[e, g][:].rearrange("p (t m u j) -> p m j u t", t=PACK, u=2, j=PACK),
                w1_raw[e, g][:].rearrange("p j (m u t) -> p m j u t", u=2, t=PACK),
            )

        def q_w1(e, g):
            w1_codes[e, g] = keep.tile([P, H], U32, name="w1c%d%d" % (e, g), align_bytes=64)
            w1_scales[e, g] = keep.tile([P, H], U8, name="w1s%d%d" % (e, g), align_bytes=64)
            quantize(w1_codes[e, g][:], w1_scales[e, g][:], w1_grouped[e, g][:])

        def il_w2(e):
            w2_grouped[e] = keep.tile([P, N, PACK], BF16, name="w2g%d" % e, align_bytes=64)
            spread(
                W2_SPLIT[e],
                w2_grouped[e][:].rearrange("p (c i) j -> p c j i", i=RUN),
                w2_raw[e][:].rearrange("p j (c i) -> p c j i", i=RUN),
            )

        def q_w2(e):
            w2_codes[e] = keep.tile([P, N], U32, name="w2c%d" % e, align_bytes=64)
            w2_scales[e] = keep.tile([P, N], U8, name="w2s%d" % e, align_bytes=64)
            quantize(w2_codes[e][:], w2_scales[e][:], w2_grouped[e][:].rearrange("p n j -> p (n j)"))

        def layer1(e, s):
            cols = slice(e * C + s * CHUNK, e * C + (s + 1) * CHUNK)
            acc[e, s] = psum.tile([P, PACK, CHUNK], F32, name="acc%d%d" % (e, s))
            for t in range(PACK):
                feats = slice(t * P, (t + 1) * P)
                for g in range(PASSES):
                    nc.tensor.matmul_mx(
                        out=acc[e, s][:, t, :],
                        lhsT=w1_codes[e, g][:, feats].bitcast(FP8X4),
                        lhsT_scale=w1_scales[e, g][:, feats],
                        rhs=x_codes[g][:, cols].bitcast(FP8X4),
                        rhs_scale=x_scales[g][:, cols],
                        start=(g == 0),
                        stop=(g == PASSES - 1),
                    )

        def gelu(e, s):
            if ("hgj", e) in YTAG:
                if e not in h_joint:
                    h_joint[e] = keep.tile([P, CHUNKS, CHUNK, PACK], BF16, name="hgj%d" % e, tag=YTAG["hgj", e], align_bytes=64)
                h_grouped[e, s] = h_joint[e][:, s]
            else:
                h_grouped[e, s] = keep.tile([P, CHUNK, PACK], BF16, name="hg%d%d" % (e, s), tag=YTAG.get(("hg", e, s), "hg%d%d" % (e, s)), align_bytes=64)
            nc.scalar.activation(out=h_grouped[e, s][:], in_=acc[e, s][:].rearrange("p t n -> p n t"), func=GELU)

        def q_h(e, s):
            cols = slice(s * CHUNK, (s + 1) * CHUNK)
            quantize(h_codes[e][:, cols], h_scales[e][:, cols], h_grouped[e, s][:].rearrange("p n t -> p (n t)"))

        def q_h_all(e):
            quantize(h_codes[e][:], h_scales[e][:], h_joint[e][:].rearrange("p s n t -> p (s n t)"))

        def layer2(e, c0, width):
            y_acc[e, c0] = psum.tile([P, N_TILES, width], F32, name="y%d%d" % (e, c0))
            for m in range(N_TILES):
                feats = slice(m * P, (m + 1) * P)
                nc.tensor.matmul_mx(
                    out=y_acc[e, c0][:, m, :],
                    lhsT=w2_codes[e][:, feats].bitcast(FP8X4),
                    lhsT_scale=w2_scales[e][:, feats],
                    rhs=h_codes[e][:, c0 : c0 + width].bitcast(FP8X4),
                    rhs_scale=h_scales[e][:, c0 : c0 + width],
                    start=True,
                    stop=True,
                )

        def y_out(e, c0, width):
            y_sb[e, c0] = keep.tile([P, N_TILES, width], F32, name="ysb%d%d" % (e, c0), tag=YTAG.get(("ysb", e, c0), "ysb%d%d" % (e, c0)), align_bytes=64)
            nc.scalar.copy(out=y_sb[e, c0][:], in_=y_acc[e, c0][:])

        def layer2_half(e, m, tag):
            feats = slice(m * P, (m + 1) * P)
            y_acc[e, m] = psum.tile([P, C], F32, name="yh%d%d" % (e, m), tag=tag)
            nc.tensor.matmul_mx(
                out=y_acc[e, m][:],
                lhsT=w2_codes[e][:, feats].bitcast(FP8X4),
                lhsT_scale=w2_scales[e][:, feats],
                rhs=h_codes[e][:].bitcast(FP8X4),
                rhs_scale=h_scales[e][:],
                start=True,
                stop=True,
            )

        def y_out_half(e, m, tag):
            y_sb[e, m] = keep.tile([P, C], F32, name="ysbh%d%d" % (e, m), tag=tag)
            nc.scalar.copy(out=y_sb[e, m][:], in_=y_acc[e, m][:])

        def scatter_half(e, m):
            nc.vector.tensor_tensor(
                out=windows[m][:].indirect(slots_of(e)),
                in0=y_sb[e, m][:],
                in1=gate_sb[e][:, m, :],
                op=MULT,
            )

        def scatter(e, c0, width):
            first = (e * C + c0) // 16
            for m in range(N_TILES):
                nc.vector.tensor_tensor(
                    out=windows[m][:].indirect(offsets[:, first : first + width // 16]),
                    in0=y_sb[e, c0][:, m, :],
                    in1=gate_sb[e][:, m, c0 : c0 + width],
                    op=MULT,
                )

        for t in range(PACK):
            v_gather(t)
            cast_plane(t)
            for e in range(E):
                s_gather(e, t)
        il_x_all()
        q_x(VPASS)
        q_x(SPASS)
        for e in range(E):
            for g in range(PASSES):
                il_w1(e, g)
                q_w1(e, g)
        for s in range(CHUNKS):
            layer1(0, s)
            gelu(0, s)
        q_h_all(0)
        for e in range(E):
            il_w2(e)
            q_w2(e)
        layer2_half(0, 0, "yh00")
        y_out_half(0, 0, "w2raw1")
        for s in range(CHUNKS):
            layer1(1, s)
            gelu(1, s)
        q_h_all(1)
        layer2_half(0, 1, "acc11")
        y_out_half(0, 1, "ysbh01")
        layer2(1, 0, C)
        y_out(1, 0, C)
        scatter_half(0, 0)
        scatter_half(0, 1)
        scatter(1, 0, C)

        for m in range(N_TILES):
            nc.sync.dma_start(out[m * P : (m + 1) * P, :], windows[m][:])
